import numpy as np
import ml_dtypes


def mxq(x, axis, fmt="e4m3"):
    dtype, down = {"e4m3": (ml_dtypes.float8_e4m3fn, 7), "e5m2": (ml_dtypes.float8_e5m2, 14)}[fmt]
    v = np.moveaxis(np.asarray(x, np.float32).astype(ml_dtypes.bfloat16).astype(np.float64), axis, -1)
    blocks = v.reshape(v.shape[:-1] + (-1, 32))
    amax = np.abs(blocks).max(-1, keepdims=True)
    byte = np.maximum(np.where(amax > 0, np.frexp(amax)[1] - 1 + 127, 0) - down, 1)
    scale = np.exp2(byte - 127.0)
    codes = (blocks / scale).astype(np.float32).astype(dtype).astype(np.float64)
    return np.moveaxis((codes * scale).reshape(v.shape), -1, axis)


WIDE = False


def mx_kscale(k):
    if not WIDE:
        return np.ones(k)
    levels = np.array([10, -10, 5, -5, 0])
    if k % 512:
        return np.exp2(np.random.permutation(np.resize(levels, k // 32))).repeat(32)
    a = np.empty((k // 512, 16))
    for p in range(k // 512):
        a[p, :8] = np.random.permutation(np.resize(levels, 8))
        for g in range(8):
            far = levels[np.abs(levels - a[p, g]) >= 10]
            a[p, g + 8] = far[np.random.randint(len(far))]
    return np.exp2(a.ravel()).repeat(32)


def f64(x):
    return np.asarray(x).astype(np.float64)


def striped8(idx):
    return np.concatenate([v.reshape(-1, 16).T for v in idx]).astype(np.uint16)


def unstriped8(offs):
    return np.stack([offs[16 * g:16 * g + 16].T.reshape(-1) for g in range(8)]).astype(np.int64)


E2M1 = np.array([0.0, 0.5, 1.0, 1.5, 2.0, 3.0, 4.0, 6.0, -0.0, -0.5, -1.0, -1.5, -2.0, -3.0, -4.0, -6.0])


def pack_weight(w, fmt):
    k, n = w.shape
    w = f64(np.asarray(w, np.float32).astype(ml_dtypes.bfloat16)).reshape(k // 32, 32, n)
    amax = np.abs(w).max(1)
    if fmt == "e4m3":
        byte = np.frexp(amax)[1] - 1 + 127 - 7
    else:
        mant, ex = np.frexp(amax / 6.0)
        byte = np.where(mant > 0.5, ex, ex - 1) + 127
    byte = np.clip(np.where(amax > 0, byte, 1), 1, 254)
    scaled = (w * np.exp2(127.0 - byte)[:, None, :]).reshape(k, n).astype(np.float32)
    by_word = np.ascontiguousarray(scaled.reshape(k // 512, 128, 4, n).transpose(0, 1, 3, 2))
    if fmt == "e4m3":
        words = by_word.astype(ml_dtypes.float8_e4m3fn).view(np.uint8)
    else:
        c = by_word.astype(ml_dtypes.float4_e2m1fn).view(np.uint8) & 0xF
        words = (c[..., 0::2] | (c[..., 1::2] << 4)).reshape(k // 512, 128, 2 * n)
    return np.ascontiguousarray(words), np.ascontiguousarray(byte.astype(np.uint8).reshape(k // 512, 16, n))


def unpack_weight(words, scales, fmt):
    g, _, n = scales.shape
    words = np.ascontiguousarray(words).reshape(g, 128, n, -1)
    if fmt == "e4m3":
        vals = words.view(ml_dtypes.float8_e4m3fn).astype(np.float64)
    else:
        nib = np.empty((g, 128, n, 4), np.uint8)
        nib[..., 0::2] = words & 0xF
        nib[..., 1::2] = words >> 4
        vals = E2M1[nib]
    vals = vals * np.repeat(np.exp2(scales.astype(np.float64) - 127.0), 8, axis=1)[..., None]
    return vals.transpose(0, 1, 3, 2).reshape(g * 512, n)


def silu(v):
    return v / (1.0 + np.exp(-np.maximum(v, -700.0)))


K, M, T, S = 1536, 128, 2048, 1024


def setup_inputs():
    n = np.random.standard_normal
    s = mx_kscale(K)[:, None]
    p_w = pack_weight(n((K, M)) / np.sqrt(K) / s, "e2m1")
    return {
        "xT": (n((K, T)) * s).astype(np.float32),
        "w_words": p_w[0],
        "w_scales": p_w[1],
        "wgt": np.repeat(np.random.uniform(0.5, 2.0, (8, S)), 16, axis=0).astype(np.float32),
        "b": (0.3 * n(128)).astype(np.float32),
        "offs": striped8(np.stack([np.random.permutation(T)[:S] for _ in range(8)])),
    }


def reference(xT, w_words, w_scales, wgt, b, offs):
    idx = unstriped8(offs)
    group = np.arange(K) % 512 // 64
    xg = f64(wgt)[np.arange(K) // 4 % 128] * f64(xT)[np.arange(K)[:, None], idx[group]]
    xT_ = mxq(xg, 0, "e4m3")
    w_ = unpack_weight(w_words, w_scales, "e2m1")
    y = w_.T @ xT_
    return silu(y + f64(b)[:, None])

@@ -1,0 +1,127 @@
+from contextlib import ExitStack
+
+import concourse.mybir as mybir
+
+K, M, T, S = 1536, 128, 2048, 1024
+P = 128
+PACK = 4
+K_PASS = P * PACK
+PASSES = K // K_PASS
+
+FLOPS = 2 * K * M * S
+
+F32 = mybir.dt.float32
+BF16 = mybir.dt.bfloat16
+I32 = mybir.dt.int32
+U32 = mybir.dt.uint32
+U16 = mybir.dt.uint16
+U8 = mybir.dt.uint8
+E4M3X4 = mybir.dt.float8_e4m3fn_x4
+E2M1X4 = mybir.dt.float4_e2m1fn_x4
+MULT = mybir.AluOpType.mult
+SILU = mybir.ActivationFunctionType.Silu
+
+HALVES = [(0, 512), (512, 512)]
+CHUNKS = [HALVES, HALVES, [(0, 512), (512, 256), (768, 128), (896, 128)]]
+GROUPS = [(0, 512), (512, 128), (640, 128), (768, 128), (896, 128)]
+
+
+def tile_list_heads_silu_kernel(tc, xT, w_words, w_scales, wgt, b, offs, out):
+    nc = tc.nc
+    with ExitStack() as ctx:
+        held = ctx.enter_context(tc.tile_pool(name="held", bufs=1))
+        ring = ctx.enter_context(tc.tile_pool(name="ring", bufs=3))
+        psum = ctx.enter_context(tc.psum_pool(name="psum", bufs=1))
+
+        lists = held.tile([P, S // 16], U16, name="lists")
+        factors = held.tile([P, S], F32, name="factors")
+        planes = [held.tile([P, T], F32, name=f"plane{n}") for n in range(PASSES * PACK)]
+        words = held.tile([P, PASSES, 2 * M], U8, name="words", align_bytes=64)
+        wscales = held.tile([P, PASSES, M], U8, name="wscales", align_bytes=64)
+        bias = held.tile([P, 1], F32, name="bias")
+        warm = held.tile([P, 1], F32, name="warm")
+        codes = held.tile([P, PASSES, S], U32, name="codes", align_bytes=64)
+        scales = held.tile([P, PASSES, S], U8, name="scales", align_bytes=64)
+        result = held.tile([P, S], F32, name="result")
+        sums = [psum.tile([P, width], F32, name=f"sum{first}") for first, width in GROUPS]
+
+        nc.vector.memset(warm[:], 0.0)
+        nc.scalar.activation(warm[:], warm[:], SILU)
+        nc.vector.memset(wscales[:].rearrange("p a n -> p (a n)").bitcast(I32), 0)
+
+        rows = xT.rearrange("(a p i) t -> a i p t", p=P, i=PACK)
+        nc.sync.dma_start(lists[:], offs)
+        nc.sync.dma_start(factors[:, 0:512], wgt[:, 0:512])
+        for n in range(PASSES * PACK):
+            nc.sync.dma_start(planes[n][:], rows[n // PACK, n % PACK])
+            if n == 0:
+                nc.sync.dma_start(factors[:, 512:1024], wgt[:, 512:1024])
+            if n == 5:
+                nc.sync.dma_start(words[:].bitcast(I32), w_words.bitcast(I32).rearrange("a p n -> p a n"))
+                for q in range(4):
+                    nc.sync.dma_start(
+                        wscales[32 * q : 32 * q + 4].bitcast(I32),
+                        w_scales.bitcast(I32)[:, 4 * q : 4 * q + 4].rearrange("a r n -> r a n"),
+                    )
+                nc.sync.dma_start(bias[:], b.unsqueeze(1))
+
+        def gather(a, first, width):
+            picked = ring.tile([P, PACK, width], F32, name=f"picked{width}")
+            for i in range(PACK):
+                nc.vector.tensor_tensor(
+                    picked[:, i, :],
+                    planes[PACK * a + i][:].indirect(lists[:, first // 16 : (first + width) // 16]),
+                    factors[:, first : first + width],
+                    MULT,
+                )
+            grouped = ring.tile([P, width, PACK], BF16, name=f"grouped{width}", align_bytes=64)
+            nc.scalar.copy(
+                grouped[:].rearrange("p (c i) t -> p c t i", i=4),
+                picked[:].rearrange("p t (c i) -> p c t i", i=4),
+            )
+            return grouped
+
+        def quantise(a, first, width, grouped):
+            nc.vector.quantize_mx(
+                out=codes[:, a, first : first + width].bitcast(E4M3X4),
+                scales=scales[:, a, first : first + width],
+                in_=grouped[:].rearrange("p c t -> p (c t)"),
+            )
+
+        def multiply(a, first, width):
+            for g, (g_first, g_width) in enumerate(GROUPS):
+                if first <= g_first and g_first + g_width <= first + width:
+                    cols = slice(g_first, g_first + g_width)
+                    nc.tensor.matmul_mx(
+                        out=sums[g][:],
+                        lhsT=words[:, a, :].bitcast(E2M1X4),
+                        lhsT_scale=wscales[:, a, :],
+                        rhs=codes[:, a, cols].bitcast(E4M3X4),
+                        rhs_scale=scales[:, a, cols],
+                        start=(a == 0),
+                        stop=(a == PASSES - 1),
+                    )
+
+        def finish(first, width):
+            for g, (g_first, g_width) in enumerate(GROUPS):
+                if first <= g_first and g_first + g_width <= first + width:
+                    nc.scalar.activation(result[:, g_first : g_first + g_width], sums[g][:], SILU, bias=bias[:])
+            nc.sync.dma_start(out[:, first : first + width], result[:, first : first + width])
+
+        jobs = [(a, first, width) for a in range(PASSES) for first, width in CHUNKS[a]]
+        pending = []
+
+        def settle():
+            job, grouped = pending[0]
+            pending.remove(pending[0])
+            quantise(*job, grouped)
+            multiply(*job)
+            if job[0] == PASSES - 1:
+                finish(job[1], job[2])
+
+        for job in jobs:
+            grouped = gather(*job)
+            pending.append((job, grouped))
+            if len(pending) > 1:
+                settle()
+        settle()

@@ -22,7 +22,7 @@ MULT = mybir.AluOpType.mult
 SILU = mybir.ActivationFunctionType.Silu
 
 HALVES = [(0, 512), (512, 512)]
-CHUNKS = [HALVES, HALVES, [(0, 512), (512, 256), (768, 128), (896, 128)]]
+LAST = [(0, 640), (640, 256), (896, 128)]
 GROUPS = [(0, 512), (512, 128), (640, 128), (768, 128), (896, 128)]
 
 
@@ -30,11 +30,14 @@ def tile_list_heads_silu_kernel(tc, xT, w_words, w_scales, wgt, b, offs, out):
     nc = tc.nc
     with ExitStack() as ctx:
         held = ctx.enter_context(tc.tile_pool(name="held", bufs=1))
-        ring = ctx.enter_context(tc.tile_pool(name="ring", bufs=3))
+        ring = ctx.enter_context(tc.tile_pool(name="ring", bufs=2))
         psum = ctx.enter_context(tc.psum_pool(name="psum", bufs=1))
 
         lists = held.tile([P, S // 16], U16, name="lists")
-        factors = held.tile([P, S], F32, name="factors")
+        factors = held.tile([P, S], F32, name="factors", align_bytes=64)
+        compact = held.tile([P, 2, 32], F32, name="compact", align_bytes=64)
+        turned = held.tile([P, 2, 32], F32, name="turned", align_bytes=64)
+        spread = held.tile([P, 32, 2, 16], F32, name="spread", align_bytes=64)
         planes = [held.tile([P, T], F32, name=f"plane{n}") for n in range(PASSES * PACK)]
         words = held.tile([P, PASSES, 2 * M], U8, name="words", align_bytes=64)
         wscales = held.tile([P, PASSES, M], U8, name="wscales", align_bytes=64)
@@ -50,12 +53,12 @@ def tile_list_heads_silu_kernel(tc, xT, w_words, w_scales, wgt, b, offs, out):
         nc.vector.memset(wscales[:].rearrange("p a n -> p (a n)").bitcast(I32), 0)
 
         rows = xT.rearrange("(a p i) t -> a i p t", p=P, i=PACK)
+        by_block = wgt.rearrange("(q g s) (b r) -> q s b g r", q=4, g=2, b=32)
+        for q in range(4):
+            nc.sync.dma_start(compact[32 * q : 32 * q + 32], by_block[q, 0])
         nc.sync.dma_start(lists[:], offs)
-        nc.sync.dma_start(factors[:, 0:512], wgt[:, 0:512])
         for n in range(PASSES * PACK):
             nc.sync.dma_start(planes[n][:], rows[n // PACK, n % PACK])
-            if n == 0:
-                nc.sync.dma_start(factors[:, 512:1024], wgt[:, 512:1024])
             if n == 5:
                 nc.sync.dma_start(words[:].bitcast(I32), w_words.bitcast(I32).rearrange("a p n -> p a n"))
                 for q in range(4):
@@ -65,63 +68,109 @@ def tile_list_heads_silu_kernel(tc, xT, w_words, w_scales, wgt, b, offs, out):
                     )
                 nc.sync.dma_start(bias[:], b.unsqueeze(1))
 
-        def gather(a, first, width):
-            picked = ring.tile([P, PACK, width], F32, name=f"picked{width}")
-            for i in range(PACK):
-                nc.vector.tensor_tensor(
-                    picked[:, i, :],
-                    planes[PACK * a + i][:].indirect(lists[:, first // 16 : (first + width) // 16]),
-                    factors[:, first : first + width],
-                    MULT,
-                )
-            grouped = ring.tile([P, width, PACK], BF16, name=f"grouped{width}", align_bytes=64)
-            nc.scalar.copy(
-                grouped[:].rearrange("p (c i) t -> p c t i", i=4),
-                picked[:].rearrange("p t (c i) -> p c t i", i=4),
+        for g in range(2):
+            nc.vector.transpose(turned[:, g, :], compact[:, g, :])
+        for half, engine in enumerate((nc.vector.tensor_copy, nc.scalar.copy)):
+            blocks = slice(16 * half, 16 * half + 16)
+            engine(
+                spread[:, blocks],
+                turned[:, :, blocks].rearrange("p g b -> p b g").unsqueeze(3).to_broadcast([P, 16, 2, 16]),
             )
-            return grouped
+        for half in range(2):
+            nc.vector.transpose(
+                factors[:, 512 * half : 512 * half + 512],
+                spread[:, 16 * half : 16 * half + 16].rearrange("p b g s -> p (b g s)"),
+            )
 
-        def quantise(a, first, width, grouped):
+        def gather(picked, a, i, first, width):
+            nc.vector.tensor_tensor(
+                picked[:, i, :],
+                planes[PACK * a + i][:].indirect(lists[:, first // 16 : (first + width) // 16]),
+                factors[:, first : first + width],
+                MULT,
+            )
+
+        def interleave(copy, grouped, picked):
+            copy(
+                grouped.rearrange("p (c i) t -> p c t i", i=4),
+                picked.rearrange("p t (c i) -> p c t i", i=4),
+            )
+
+        def quantise(a, first, grouped):
+            cols = slice(first, first + grouped.shape[1])
             nc.vector.quantize_mx(
-                out=codes[:, a, first : first + width].bitcast(E4M3X4),
-                scales=scales[:, a, first : first + width],
-                in_=grouped[:].rearrange("p c t -> p (c t)"),
+                out=codes[:, a, cols].bitcast(E4M3X4),
+                scales=scales[:, a, cols],
+                in_=grouped.rearrange("p c t -> p (c t)"),
             )
 
-        def multiply(a, first, width):
-            for g, (g_first, g_width) in enumerate(GROUPS):
-                if first <= g_first and g_first + g_width <= first + width:
-                    cols = slice(g_first, g_first + g_width)
-                    nc.tensor.matmul_mx(
-                        out=sums[g][:],
-                        lhsT=words[:, a, :].bitcast(E2M1X4),
-                        lhsT_scale=wscales[:, a, :],
-                        rhs=codes[:, a, cols].bitcast(E4M3X4),
-                        rhs_scale=scales[:, a, cols],
-                        start=(a == 0),
-                        stop=(a == PASSES - 1),
-                    )
+        def multiply(a, groups):
+            for g in groups:
+                first, width = GROUPS[g]
+                cols = slice(first, first + width)
+                nc.tensor.matmul_mx(
+                    out=sums[g][:],
+                    lhsT=words[:, a, :].bitcast(E2M1X4),
+                    lhsT_scale=wscales[:, a, :],
+                    rhs=codes[:, a, cols].bitcast(E4M3X4),
+                    rhs_scale=scales[:, a, cols],
+                    start=(a == 0),
+                    stop=(a == PASSES - 1),
+                )
 
-        def finish(first, width):
-            for g, (g_first, g_width) in enumerate(GROUPS):
-                if first <= g_first and g_first + g_width <= first + width:
-                    nc.scalar.activation(result[:, g_first : g_first + g_width], sums[g][:], SILU, bias=bias[:])
-            nc.sync.dma_start(out[:, first : first + width], result[:, first : first + width])
+        def finish(groups, queue):
+            for g in groups:
+                first, width = GROUPS[g]
+                nc.scalar.activation(result[:, first : first + width], sums[g][:], SILU, bias=bias[:])
+            begin, end = GROUPS[groups[0]][0], sum(GROUPS[groups[-1]])
+            queue.dma_start(out[:, begin:end], result[:, begin:end])
 
-        jobs = [(a, first, width) for a in range(PASSES) for first, width in CHUNKS[a]]
-        pending = []
+        late = []
 
         def settle():
-            job, grouped = pending[0]
-            pending.remove(pending[0])
-            quantise(*job, grouped)
-            multiply(*job)
-            if job[0] == PASSES - 1:
-                finish(job[1], job[2])
+            for a, grouped in late:
+                quantise(a, 0, grouped[:])
+                multiply(a, range(len(GROUPS)))
+            late.clear()
 
-        for job in jobs:
-            grouped = gather(*job)
-            pending.append((job, grouped))
-            if len(pending) > 1:
+        for a in range(PASSES - 1):
+            picked = [ring.tile([P, PACK, width], F32, name=f"picked{first}") for first, width in HALVES]
+            for i in range(PACK):
+                for h, (first, width) in enumerate(HALVES):
+                    gather(picked[h], a, i, first, width)
+                if i == 2:
+                    settle()
+            grouped = ring.tile([P, S, PACK], BF16, name="grouped", align_bytes=64)
+            for h, (first, width) in enumerate(HALVES):
+                interleave(nc.scalar.copy, grouped[:, first : first + width], picked[h][:])
+            late.append((a, grouped))
+
+        a = PASSES - 1
+        picked = [held.tile([P, PACK, width], F32, name=f"last_picked{first}") for first, width in LAST]
+        grouped = held.tile([P, S, PACK], BF16, name="last_grouped", align_bytes=64)
+        for i in range(PACK):
+            gather(picked[0], a, i, *LAST[0])
+            if i == 2:
                 settle()
-        settle()
+        interleave(nc.scalar.copy, grouped[:, 0:512], picked[0][:, :, 0:512])
+        interleave(nc.scalar.copy, grouped[:, 512:640], picked[0][:, :, 512:640])
+        for i in range(PACK):
+            if i == 3:
+                quantise(a, 0, grouped[:, 0:512])
+                multiply(a, [0])
+            gather(picked[1], a, i, *LAST[1])
+        interleave(nc.scalar.copy, grouped[:, 640:896], picked[1][:])
+        quantise(a, 512, grouped[:, 512:640])
+        multiply(a, [1])
+        for i in range(PACK):
+            if i == 3:
+                quantise(a, 640, grouped[:, 640:896])
+                multiply(a, [2, 3])
+            gather(picked[2], a, i, *LAST[2])
+        finish([0], nc.sync)
+        finish([1], nc.sync)
+        interleave(nc.vector.tensor_copy, grouped[:, 896:1024], picked[2][:])
+        finish([2, 3], nc.sync)
+        quantise(a, 896, grouped[:, 896:1024])
+        multiply(a, [4])
+        finish([4], nc.scalar)

@@ -21,8 +21,6 @@ E2M1X4 = mybir.dt.float4_e2m1fn_x4
 MULT = mybir.AluOpType.mult
 SILU = mybir.ActivationFunctionType.Silu
 
-HALVES = [(0, 512), (512, 512)]
-LAST = [(0, 640), (640, 256), (896, 128)]
 GROUPS = [(0, 512), (512, 128), (640, 128), (768, 128), (896, 128)]
 
 
@@ -30,7 +28,6 @@ def tile_list_heads_silu_kernel(tc, xT, w_words, w_scales, wgt, b, offs, out):
     nc = tc.nc
     with ExitStack() as ctx:
         held = ctx.enter_context(tc.tile_pool(name="held", bufs=1))
-        ring = ctx.enter_context(tc.tile_pool(name="ring", bufs=2))
         psum = ctx.enter_context(tc.psum_pool(name="psum", bufs=1))
 
         lists = held.tile([P, S // 16], U16, name="lists")
@@ -48,15 +45,15 @@ def tile_list_heads_silu_kernel(tc, xT, w_words, w_scales, wgt, b, offs, out):
         result = held.tile([P, S], F32, name="result")
         sums = [psum.tile([P, width], F32, name=f"sum{first}") for first, width in GROUPS]
 
-        nc.vector.memset(warm[:], 0.0)
-        nc.scalar.activation(warm[:], warm[:], SILU)
-        nc.vector.memset(wscales[:].rearrange("p a n -> p (a n)").bitcast(I32), 0)
-
         rows = xT.rearrange("(a p i) t -> a i p t", p=P, i=PACK)
         by_block = wgt.rearrange("(q g s) (b r) -> q s b g r", q=4, g=2, b=32)
         for q in range(4):
-            nc.sync.dma_start(compact[32 * q : 32 * q + 32], by_block[q, 0])
+            queue = nc.sync if q < 2 else nc.scalar
+            queue.dma_start(compact[32 * q : 32 * q + 32], by_block[q, 0])
         nc.sync.dma_start(lists[:], offs)
+        nc.vector.memset(warm[:], 0.0)
+        nc.scalar.activation(warm[:], warm[:], SILU)
+        nc.vector.memset(wscales[:].rearrange("p a n -> p (a n)").bitcast(I32), 0)
         for n in range(PASSES * PACK):
             nc.sync.dma_start(planes[n][:], rows[n // PACK, n % PACK])
             if n == 5:
@@ -76,13 +73,15 @@ def tile_list_heads_silu_kernel(tc, xT, w_words, w_scales, wgt, b, offs, out):
                 spread[:, blocks],
                 turned[:, :, blocks].rearrange("p g b -> p b g").unsqueeze(3).to_broadcast([P, 16, 2, 16]),
             )
-        for half in range(2):
+
+        def spread_factors(half):
             nc.vector.transpose(
                 factors[:, 512 * half : 512 * half + 512],
                 spread[:, 16 * half : 16 * half + 16].rearrange("p b g s -> p (b g s)"),
             )
 
-        def gather(picked, a, i, first, width):
+        def gather(slab, i):
+            a, first, width, picked, grouped = slab
             nc.vector.tensor_tensor(
                 picked[:, i, :],
                 planes[PACK * a + i][:].indirect(lists[:, first // 16 : (first + width) // 16]),
@@ -90,18 +89,18 @@ def tile_list_heads_silu_kernel(tc, xT, w_words, w_scales, wgt, b, offs, out):
                 MULT,
             )
 
-        def interleave(copy, grouped, picked):
+        def interleave(copy, slab, begin, end):
+            a, first, width, picked, grouped = slab
             copy(
-                grouped.rearrange("p (c i) t -> p c t i", i=4),
-                picked.rearrange("p t (c i) -> p c t i", i=4),
+                grouped[:, first + begin : first + end].rearrange("p (c i) t -> p c t i", i=4),
+                picked[:, :, begin:end].rearrange("p t (c i) -> p c t i", i=4),
             )
 
-        def quantise(a, first, grouped):
-            cols = slice(first, first + grouped.shape[1])
+        def quantise(a, begin, end):
             nc.vector.quantize_mx(
-                out=codes[:, a, cols].bitcast(E4M3X4),
-                scales=scales[:, a, cols],
-                in_=grouped.rearrange("p c t -> p (c t)"),
+                out=codes[:, a, begin:end].bitcast(E4M3X4),
+                scales=scales[:, a, begin:end],
+                in_=passes[a][:, begin:end].rearrange("p c t -> p (c t)"),
             )
 
         def multiply(a, groups):
@@ -125,52 +124,64 @@ def tile_list_heads_silu_kernel(tc, xT, w_words, w_scales, wgt, b, offs, out):
             begin, end = GROUPS[groups[0]][0], sum(GROUPS[groups[-1]])
             queue.dma_start(out[:, begin:end], result[:, begin:end])
 
-        late = []
+        passes = [held.tile([P, S, PACK], BF16, name=f"grouped{a}", align_bytes=64) for a in range(PASSES)]
 
-        def settle():
-            for a, grouped in late:
-                quantise(a, 0, grouped[:])
-                multiply(a, range(len(GROUPS)))
-            late.clear()
+        def slab(a, first, width):
+            picked = held.tile([P, PACK, width], F32, name=f"picked{a}_{first}")
+            return a, first, width, picked, passes[a]
 
-        for a in range(PASSES - 1):
-            picked = [ring.tile([P, PACK, width], F32, name=f"picked{first}") for first, width in HALVES]
-            for i in range(PACK):
-                for h, (first, width) in enumerate(HALVES):
-                    gather(picked[h], a, i, first, width)
-                if i == 2:
-                    settle()
-            grouped = ring.tile([P, S, PACK], BF16, name="grouped", align_bytes=64)
-            for h, (first, width) in enumerate(HALVES):
-                interleave(nc.scalar.copy, grouped[:, first : first + width], picked[h][:])
-            late.append((a, grouped))
+        s00, s01 = slab(0, 0, 512), slab(0, 512, 512)
+        s10, s11 = slab(1, 0, 512), slab(1, 512, 512)
+        s20, s21, s22 = slab(2, 0, 640), slab(2, 640, 256), slab(2, 896, 128)
+        on_scalar, on_vector = nc.scalar.copy, nc.vector.tensor_copy
 
-        a = PASSES - 1
-        picked = [held.tile([P, PACK, width], F32, name=f"last_picked{first}") for first, width in LAST]
-        grouped = held.tile([P, S, PACK], BF16, name="last_grouped", align_bytes=64)
         for i in range(PACK):
-            gather(picked[0], a, i, *LAST[0])
-            if i == 2:
-                settle()
-        interleave(nc.scalar.copy, grouped[:, 0:512], picked[0][:, :, 0:512])
-        interleave(nc.scalar.copy, grouped[:, 512:640], picked[0][:, :, 512:640])
-        for i in range(PACK):
-            if i == 3:
-                quantise(a, 0, grouped[:, 0:512])
-                multiply(a, [0])
-            gather(picked[1], a, i, *LAST[1])
-        interleave(nc.scalar.copy, grouped[:, 640:896], picked[1][:])
-        quantise(a, 512, grouped[:, 512:640])
-        multiply(a, [1])
-        for i in range(PACK):
-            if i == 3:
-                quantise(a, 640, grouped[:, 640:896])
-                multiply(a, [2, 3])
-            gather(picked[2], a, i, *LAST[2])
+            for h, s in enumerate((s00, s01)):
+                if i == 0:
+                    spread_factors(h)
+                gather(s, i)
+        interleave(on_scalar, s00, 0, 512)
+        interleave(on_scalar, s01, 0, 512)
+
+        for i in range(3):
+            gather(s10, i)
+            gather(s11, i)
+        quantise(0, 0, 1024)
+        multiply(0, [0, 1, 2, 3, 4])
+        gather(s10, 3)
+        interleave(on_scalar, s10, 0, 512)
+
+        gather(s20, 0)
+        gather(s20, 1)
+        quantise(1, 0, 512)
+        multiply(1, [0])
+        gather(s20, 2)
+        gather(s20, 3)
+        interleave(on_scalar, s20, 0, 512)
+        interleave(on_scalar, s20, 512, 640)
+        gather(s11, 3)
+        interleave(on_scalar, s11, 0, 512)
+
+        for i in range(3):
+            gather(s21, i)
+        quantise(2, 0, 512)
+        multiply(2, [0])
+        gather(s21, 3)
+        interleave(on_scalar, s21, 0, 256)
         finish([0], nc.sync)
+        quantise(2, 512, 640)
+        gather(s22, 0)
+        gather(s22, 1)
+        quantise(1, 512, 1024)
+        multiply(1, [1, 2, 3, 4])
+        multiply(2, [1])
+        gather(s22, 2)
+        quantise(2, 640, 896)
+        multiply(2, [2, 3])
+        gather(s22, 3)
         finish([1], nc.sync)
-        interleave(nc.vector.tensor_copy, grouped[:, 896:1024], picked[2][:])
+        interleave(on_vector, s22, 0, 128)
         finish([2, 3], nc.sync)
-        quantise(a, 896, grouped[:, 896:1024])
-        multiply(a, [4])
+        quantise(2, 896, 1024)
+        multiply(2, [4])
         finish([4], nc.scalar)

@@ -143,43 +143,39 @@ def tile_list_heads_silu_kernel(tc, xT, w_words, w_scales, wgt, b, offs, out):
         interleave(on_scalar, s00, 0, 512)
         interleave(on_scalar, s01, 0, 512)
 
-        for i in range(3):
+        for i in range(PACK):
             gather(s10, i)
             gather(s11, i)
-        quantise(0, 0, 1024)
-        multiply(0, [0, 1, 2, 3, 4])
-        gather(s10, 3)
+            if i == 2:
+                quantise(0, 0, 1024)
+                multiply(0, [0, 1, 2, 3, 4])
         interleave(on_scalar, s10, 0, 512)
-
-        gather(s20, 0)
-        gather(s20, 1)
-        quantise(1, 0, 512)
-        multiply(1, [0])
-        gather(s20, 2)
-        gather(s20, 3)
-        interleave(on_scalar, s20, 0, 512)
-        interleave(on_scalar, s20, 512, 640)
-        gather(s11, 3)
         interleave(on_scalar, s11, 0, 512)
 
         for i in range(3):
-            gather(s21, i)
+            gather(s20, i)
+        gather(s21, 0)
+        quantise(1, 0, 1024)
+        multiply(1, [0, 1, 2, 3, 4])
+        gather(s20, 3)
+        interleave(on_scalar, s20, 0, 512)
+        interleave(on_scalar, s20, 512, 640)
+
+        gather(s21, 1)
+        gather(s21, 2)
         quantise(2, 0, 512)
         multiply(2, [0])
         gather(s21, 3)
         interleave(on_scalar, s21, 0, 256)
         finish([0], nc.sync)
         quantise(2, 512, 640)
-        gather(s22, 0)
-        gather(s22, 1)
-        quantise(1, 512, 1024)
-        multiply(1, [1, 2, 3, 4])
         multiply(2, [1])
-        gather(s22, 2)
+        for i in range(3):
+            gather(s22, i)
+        finish([1], nc.sync)
         quantise(2, 640, 896)
         multiply(2, [2, 3])
         gather(s22, 3)
-        finish([1], nc.sync)
         interleave(on_vector, s22, 0, 128)
         finish([2, 3], nc.sync)
         quantise(2, 896, 1024)

from contextlib import ExitStack

import concourse.mybir as mybir

K, M, T, S = 1536, 128, 2048, 1024
P = 128
PACK = 4
K_PASS = P * PACK
PASSES = K // K_PASS

FLOPS = 2 * K * M * S

F32 = mybir.dt.float32
BF16 = mybir.dt.bfloat16
I32 = mybir.dt.int32
U32 = mybir.dt.uint32
U16 = mybir.dt.uint16
U8 = mybir.dt.uint8
E4M3X4 = mybir.dt.float8_e4m3fn_x4
E2M1X4 = mybir.dt.float4_e2m1fn_x4
MULT = mybir.AluOpType.mult
SILU = mybir.ActivationFunctionType.Silu

GROUPS = [(0, 512), (512, 128), (640, 128), (768, 128), (896, 128)]


def tile_list_heads_silu_kernel(tc, xT, w_words, w_scales, wgt, b, offs, out):
    nc = tc.nc
    with ExitStack() as ctx:
        held = ctx.enter_context(tc.tile_pool(name="held", bufs=1))
        psum = ctx.enter_context(tc.psum_pool(name="psum", bufs=1))

        lists = held.tile([P, S // 16], U16, name="lists")
        factors = held.tile([P, S], F32, name="factors", align_bytes=64)
        compact = held.tile([P, 2, 32], F32, name="compact", align_bytes=64)
        turned = held.tile([P, 2, 32], F32, name="turned", align_bytes=64)
        spread = held.tile([P, 32, 2, 16], F32, name="spread", align_bytes=64)
        planes = [held.tile([P, T], F32, name=f"plane{n}") for n in range(PASSES * PACK)]
        words = held.tile([P, PASSES, 2 * M], U8, name="words", align_bytes=64)
        wscales = held.tile([P, PASSES, M], U8, name="wscales", align_bytes=64)
        bias = held.tile([P, 1], F32, name="bias")
        warm = held.tile([P, 1], F32, name="warm")
        codes = held.tile([P, PASSES, S], U32, name="codes", align_bytes=64)
        scales = held.tile([P, PASSES, S], U8, name="scales", align_bytes=64)
        result = held.tile([P, S], F32, name="result")
        sums = [psum.tile([P, width], F32, name=f"sum{first}") for first, width in GROUPS]

        rows = xT.rearrange("(a p i) t -> a i p t", p=P, i=PACK)
        by_block = wgt.rearrange("(q g s) (b r) -> q s b g r", q=4, g=2, b=32)
        for q in range(4):
            queue = nc.sync if q < 2 else nc.scalar
            queue.dma_start(compact[32 * q : 32 * q + 32], by_block[q, 0])
        nc.sync.dma_start(lists[:], offs)
        nc.vector.memset(warm[:], 0.0)
        nc.scalar.activation(warm[:], warm[:], SILU)
        nc.vector.memset(wscales[:].rearrange("p a n -> p (a n)").bitcast(I32), 0)
        for n in range(PASSES * PACK):
            nc.sync.dma_start(planes[n][:], rows[n // PACK, n % PACK])
            if n == 5:
                nc.sync.dma_start(words[:].bitcast(I32), w_words.bitcast(I32).rearrange("a p n -> p a n"))
                for q in range(4):
                    nc.sync.dma_start(
                        wscales[32 * q : 32 * q + 4].bitcast(I32),
                        w_scales.bitcast(I32)[:, 4 * q : 4 * q + 4].rearrange("a r n -> r a n"),
                    )
                nc.sync.dma_start(bias[:], b.unsqueeze(1))

        for g in range(2):
            nc.vector.transpose(turned[:, g, :], compact[:, g, :])
        for half, engine in enumerate((nc.vector.tensor_copy, nc.scalar.copy)):
            blocks = slice(16 * half, 16 * half + 16)
            engine(
                spread[:, blocks],
                turned[:, :, blocks].rearrange("p g b -> p b g").unsqueeze(3).to_broadcast([P, 16, 2, 16]),
            )

        def spread_factors(half):
            nc.vector.transpose(
                factors[:, 512 * half : 512 * half + 512],
                spread[:, 16 * half : 16 * half + 16].rearrange("p b g s -> p (b g s)"),
            )

        def gather(slab, i):
            a, first, width, picked, grouped = slab
            nc.vector.tensor_tensor(
                picked[:, i, :],
                planes[PACK * a + i][:].indirect(lists[:, first // 16 : (first + width) // 16]),
                factors[:, first : first + width],
                MULT,
            )

        def interleave(copy, slab, begin, end):
            a, first, width, picked, grouped = slab
            copy(
                grouped[:, first + begin : first + end].rearrange("p (c i) t -> p c t i", i=4),
                picked[:, :, begin:end].rearrange("p t (c i) -> p c t i", i=4),
            )

        def quantise(a, begin, end):
            nc.vector.quantize_mx(
                out=codes[:, a, begin:end].bitcast(E4M3X4),
                scales=scales[:, a, begin:end],
                in_=passes[a][:, begin:end].rearrange("p c t -> p (c t)"),
            )

        def multiply(a, groups):
            for g in groups:
                first, width = GROUPS[g]
                cols = slice(first, first + width)
                nc.tensor.matmul_mx(
                    out=sums[g][:],
                    lhsT=words[:, a, :].bitcast(E2M1X4),
                    lhsT_scale=wscales[:, a, :],
                    rhs=codes[:, a, cols].bitcast(E4M3X4),
                    rhs_scale=scales[:, a, cols],
                    start=(a == 0),
                    stop=(a == PASSES - 1),
                )

        def finish(groups, queue):
            for g in groups:
                first, width = GROUPS[g]
                nc.scalar.activation(result[:, first : first + width], sums[g][:], SILU, bias=bias[:])
            begin, end = GROUPS[groups[0]][0], sum(GROUPS[groups[-1]])
            queue.dma_start(out[:, begin:end], result[:, begin:end])

        passes = [held.tile([P, S, PACK], BF16, name=f"grouped{a}", align_bytes=64) for a in range(PASSES)]

        def slab(a, first, width):
            picked = held.tile([P, PACK, width], F32, name=f"picked{a}_{first}")
            return a, first, width, picked, passes[a]

        s00, s01 = slab(0, 0, 512), slab(0, 512, 512)
        s10, s11 = slab(1, 0, 512), slab(1, 512, 512)
        s20, s21, s22 = slab(2, 0, 640), slab(2, 640, 256), slab(2, 896, 128)
        on_scalar, on_vector = nc.scalar.copy, nc.vector.tensor_copy

        for i in range(PACK):
            for h, s in enumerate((s00, s01)):
                if i == 0:
                    spread_factors(h)
                gather(s, i)
        interleave(on_scalar, s00, 0, 512)
        interleave(on_scalar, s01, 0, 512)

        for i in range(PACK):
            gather(s10, i)
            gather(s11, i)
            if i == 2:
                quantise(0, 0, 1024)
                multiply(0, [0, 1, 2, 3, 4])
        interleave(on_scalar, s10, 0, 512)
        interleave(on_scalar, s11, 0, 512)

        for i in range(3):
            gather(s20, i)
        gather(s21, 0)
        quantise(1, 0, 1024)
        multiply(1, [0, 1, 2, 3, 4])
        gather(s20, 3)
        interleave(on_scalar, s20, 0, 512)
        interleave(on_scalar, s20, 512, 640)

        gather(s21, 1)
        gather(s21, 2)
        quantise(2, 0, 512)
        multiply(2, [0])
        gather(s21, 3)
        interleave(on_scalar, s21, 0, 256)
        finish([0], nc.sync)
        quantise(2, 512, 640)
        multiply(2, [1])
        for i in range(3):
            gather(s22, i)
        finish([1], nc.sync)
        quantise(2, 640, 896)
        multiply(2, [2, 3])
        gather(s22, 3)
        interleave(on_vector, s22, 0, 128)
        finish([2, 3], nc.sync)
        quantise(2, 896, 1024)
        multiply(2, [4])
        finish([4], nc.scalar)
